import numpy as np, ml_dtypes
CORES = [144,200,272,328,400,456]
N = 6
NB, B = 3, 512
def setup_inputs(rng):
    return {"x": rng.standard_normal((N, 128, NB * B), dtype=np.float32).astype(ml_dtypes.bfloat16), "wv": (rng.standard_normal((N, 128, 128), dtype=np.float32) / 16).astype(ml_dtypes.bfloat16), "wh": (rng.standard_normal((N, 128, 128), dtype=np.float32) / 16).astype(ml_dtypes.bfloat16)}
def setup_inputs_big(rng):
    d = setup_inputs(rng)
    for k in ("x",): d[k] = (d[k].astype(np.float32) * 1048576.0).astype(d[k].dtype)
    return d
def setup_inputs_small(rng):
    d = setup_inputs(rng)
    for k in ("x",): d[k] = (d[k].astype(np.float32) * (1 / 1048576.0)).astype(d[k].dtype)
    return d
def setup_inputs_apart(rng):
    d = setup_inputs(rng)
    f = (10.0 ** rng.permutation(np.linspace(-1.5, 1.5, N))).astype(np.float32).reshape(N, 1, 1)
    for k in ("x",): d[k] = (d[k].astype(np.float32) * f).astype(d[k].dtype)
    return d
def reference(x, wv, wh):
    X, WV, WH = x.astype(np.float64), wv.astype(np.float64), wh.astype(np.float64)
    h = np.zeros((N, NB, 128, B))
    for r in range(N):
        for c in range(NB):
            a = X[r][:, B * c:B * c + B].copy()
            if r: a += WV[r].T @ h[r - 1][c]
            if c: a += WH[r].T @ h[r][c - 1]
            h[r][c] = np.maximum(a, 0.0)
    return {"y": np.concatenate([h[:, c] for c in range(NB)], axis=2).astype(ml_dtypes.bfloat16)}

@@ -1,0 +1,363 @@
+from concourse.bass import DstId, RemoteDMATransfer
+from concourse.mybir import AluOpType
+
+NSIM = 512
+P, B, NB = 128, 512, 3
+K = 2
+W = B // K
+MW = W + 2 * P
+PAIRW = 2 * W + 2 * P
+RW = 2 * P + NB * W
+HUBR = (1, 2, 3, 4)
+NBANK = 8
+RELAY_ALL = False
+LANE_FWD = (0,)
+HS = 2
+HW = B // HS
+
+SCRATCH = {
+    "m0": ("sbuf", [P, (K // 2) * PAIRW], "bfloat16"),
+    "xin": ("sbuf", [P, NB * B], "bfloat16"),
+    "hprev": ("sbuf", [P, NB * B], "bfloat16"),
+    "hown": ("sbuf", [P, NB * B], "bfloat16"),
+    "ident": ("sbuf", [P, P], "bfloat16"),
+    "idsrc": ("sbuf", [P, P + 1], "bfloat16"),
+    "zeros": ("sbuf", [P, B], "bfloat16"),
+    "hubin": ("sbuf", [P, len(HUBR) * RW], "bfloat16"),
+    "hubh": ("sbuf", [P, (len(HUBR) + 1) * NB * W], "bfloat16"),
+    "idd": ("dram", [P + 1, P], "bfloat16"),
+    "ps": ("psum", [P, NBANK * 512], "float32"),
+}
+SEMAPHORES = (["ms0", "ms1", "ms2", "id1", "id2", "ldm", "ld0", "ld1", "ld2", "ah0", "ah1", "ah2", "st0", "st1", "st2", "sent"]
+              + ["ax%d%d" % (r, c) for r in range(5) for c in range(NB)]
+              + ["pe%d%d" % (r, c) for r in range(5) for c in range(NB)]
+              + ["rl%d%d" % (r, c) for r in range(5) for c in range(NB)])
+
+
+def _bits(m):
+    return [i for i in range(16) if (m >> i) & 1]
+
+
+def _mask(lst):
+    return sum(1 << i for i in lst)
+
+
+def _part(m, n, j):
+    b = _bits(m)
+    q = len(b) // n
+    return _mask(b[j * q:(j + 1) * q])
+
+
+def _chip_cores(topo, c):
+    return [d for d in range(NSIM) if topo.host(d) == topo.host(c) and topo.chip(d) == topo.chip(c)]
+
+
+def _pick(topo, cands, dies):
+    out = []
+    for d in dies:
+        out.append([c for c in cands if topo.die(c) == d and c not in out][0])
+    return out
+
+
+def _slot(b):
+    return 2 * b[1] + b[0]
+
+
+ORDER = sorted([(r, c) for r in HUBR for c in range(NB)], key=lambda b: (_slot(b), b[1]))
+SLOTS = sorted(set(_slot(b) for b in ORDER))
+
+
+def _out_masks(topo, lane, R):
+    off = topo.mask(lane, R[HUBR[-1] + 1])
+    out = dict(((0, c), off) for c in LANE_FWD)
+    for t in SLOTS:
+        bs = [b for b in ORDER if _slot(b) == t]
+        far = [b for b in bs if not (topo.mask(lane, R[b[0] + 1]) & ~off)]
+        for b in bs:
+            out[b] = _part(off, len(far), far.index(b)) if b in far else topo.mask(lane, R[b[0] + 1]) & ~off
+    return out
+
+
+def _plan(T, topo):
+    R = list(T.cores)
+    own = [c for c in _chip_cores(topo, R[2]) if c not in R and all(topo.may_write(c, R[r + 1]) for r in (0,) + HUBR)]
+    dies = sorted(set(topo.die(c) for c in own), key=lambda d: d != topo.die(R[2]))
+    lanes = _pick(topo, own, [dies[k % len(dies)] for k in range(K)])
+    relays = {}
+    for r in HUBR:
+        here = topo.host(R[r]) == topo.host(lanes[0]) and topo.chip(R[r]) == topo.chip(lanes[0])
+        if not all(topo.may_write(R[r], l) for l in lanes) or (RELAY_ALL and not here):
+            cands = [c for c in _chip_cores(topo, R[r]) if c not in R and all(topo.may_write(c, l) for l in lanes)]
+            relays[r] = _pick(topo, cands, [topo.die(l) for l in lanes])
+    pass0 = _pick(topo, [c for c in _chip_cores(topo, R[0]) if c not in R and topo.may_write(c, R[1])], [topo.die(R[0])])[0]
+    return R, lanes, relays, pass0
+
+
+def rank_program(g, core, T, topo):
+    R, lanes, relays, pass0 = _plan(T, topo)
+    S = T.sem
+    sent = [0]
+
+    def tr(dst, out_ap, in_ap, sem, mask):
+        rid, pid = topo.addr(dst, core)
+        sent[0] += len(_bits(mask))
+        return RemoteDMATransfer(dst_ids=[DstId(rid=rid, pnc=pid)], dma_engine_mask=mask, remote_sem=sem, src=in_ap, dst=out_ap)
+
+    def send(trs):
+        g.remote_dma_fused(trs, local_sem=S.sent)
+
+    def finish():
+        if sent[0]:
+            g.wait_ge(S.sent, sent[0])
+
+    def constants(q):
+        g.vector.memset(T.idsrc[:, :], 0.0).then_inc(S.ms0, 1)
+        g.vector.wait_ge(S.ms0, 1)
+        g.vector.memset(T.idsrc[:, 0:1], 1.0).then_inc(S.ms1, 1)
+        g.vector.memset(T.zeros[:, :], 0.0).then_inc(S.ms2, 1)
+        g.vector.wait_ge(S.ms2, 1)
+        q.wait_ge(S.ms1, 1)
+        q.dma_start(T.idd[:, :], T.idsrc[:, :]).then_inc(S.id1, 16)
+        q.wait_ge(S.id1, 16)
+        q.dma_start(T.ident[:, :], T.idd[0:P, :]).then_inc(S.id2, 16)
+
+    def hub_region(r):
+        return (r - 1) * RW
+
+    def msg_cols(k):
+        o = (k // 2) * PAIRW + (k % 2) * W
+        return o, o + MW
+
+    def n_in(src, dst, parts):
+        return len(_bits(topo.mask(src, dst))) // parts
+
+    for r in relays:
+        if core in relays[r]:
+            k = relays[r].index(core)
+            lane = lanes[k]
+            m = topo.mask(core, lane)
+            for c in range(NB):
+                g.wait_ge(S["ah%d" % c], n_in(R[r], core, K))
+                if c == 0:
+                    a, b = msg_cols(k)
+                    src, dst = T.m0[:, a:b], T.hubin[:, hub_region(r):hub_region(r) + MW]
+                else:
+                    o = hub_region(r) + 2 * P + c * W
+                    src, dst = T.xin[:, c * B + k * W:c * B + (k + 1) * W], T.hubin[:, o:o + W]
+                send([tr(lane, dst, src, S["ax%d%d" % (r, c)], m)])
+            finish()
+            return
+
+    if core == pass0:
+        m_in = topo.mask(R[0], core) & ~topo.mask(R[0], lanes[0])
+        for c in range(NB):
+            if c not in LANE_FWD:
+                g.wait_ge(S["ah%d" % c], len(_bits(m_in)))
+                blk = slice(c * B, (c + 1) * B)
+                send([tr(R[1], T.hprev[:, blk], T.hprev[:, blk], S["ah%d" % c], topo.mask(core, R[1]))])
+        finish()
+        return
+
+    if core in lanes:
+        k = lanes.index(core)
+        side = k % 2
+        pe, ve = g.tensor, g.vector
+        constants(g.sync)
+
+        def X(r, c):
+            o = hub_region(r) + (0 if (c == 0 and side == 0) else 2 * P + c * W)
+            return T.hubin[:, o:o + W]
+
+        def WV(r):
+            o = hub_region(r) + (W if side == 0 else 0)
+            return T.hubin[:, o:o + P]
+
+        def WH(r):
+            o = hub_region(r) + (W if side == 0 else 0) + P
+            return T.hubin[:, o:o + P]
+
+        def H(r, c):
+            o = (NB * r + c) * W
+            return T.hubh[:, o:o + W]
+
+        bank, owner, has_a = {}, [None] * NBANK, set()
+
+        def PS(b):
+            return T.ps[:, bank[b] * 512:bank[b] * 512 + W]
+
+        def n_arr(r):
+            if r in relays:
+                return len(_bits(topo.mask(relays[r][k], core)))
+            return n_in(R[r], core, K)
+
+        def emit_a(b):
+            if b in has_a:
+                return
+            has_a.add(b)
+            free = [i for i in range(NBANK) if owner[i] is None]
+            if free:
+                i = free[0]
+            else:
+                i = min(range(NBANK), key=lambda j: ORDER.index(owner[j]))
+                pe.wait_ge(S["rl%d%d" % owner[i]], 1)
+            owner[i], bank[b] = b, i
+            pe.wait_ge(S["ax%d%d" % b], n_arr(b[0]))
+            pe.matmul(PS(b), T.ident[:, :], X(*b), start=True, stop=False)
+
+        def emit_c(b):
+            r, c = b
+            if c:
+                pe.wait_ge(S["rl%d%d" % (r, c - 1)], 1)
+                pe.matmul(PS(b), WH(r), H(r, c - 1), start=False, stop=False)
+
+        def emit_b(b):
+            r, c = b
+            if r == 1:
+                pe.wait_ge(S["ax0%d" % c], n_arr(0))
+            else:
+                pe.wait_ge(S["rl%d%d" % (r - 1, c)], 1)
+            pe.matmul(PS(b), WV(r), H(r - 1, c), start=False, stop=True).then_inc(S["pe%d%d" % b], 1)
+
+        pe.wait_ge(S.id2, 16)
+        early = [(r, c) for r in HUBR if r not in relays and topo.chip(R[r]) == topo.chip(core) and topo.host(R[r]) == topo.host(core)
+                 for c in range(NB)] + [(r, 0) for r in HUBR if r not in relays]
+        for b in early:
+            emit_a(b)
+        for b in ORDER:
+            if _slot(b) == SLOTS[0]:
+                emit_a(b)
+        for t in SLOTS:
+            for b in ORDER:
+                if _slot(b) == t:
+                    emit_b(b)
+            for b in ORDER:
+                if _slot(b) == t + 1:
+                    emit_a(b)
+                    emit_c(b)
+        for b in ORDER:
+            ve.wait_ge(S["pe%d%d" % b], 1)
+            ve.tensor_tensor(out=H(*b), in0=PS(b), in1=T.zeros[:, 0:W], op=AluOpType.max).then_inc(S["rl%d%d" % b], 1)
+        om = _out_masks(topo, core, R)
+
+        def out(r, c):
+            return tr(R[r + 1], T.hprev[:, c * B + k * W:c * B + (k + 1) * W], H(r, c), S["ah%d" % c], om[(r, c)])
+
+        for c in LANE_FWD:
+            g.wait_ge(S["ax0%d" % c], n_arr(0))
+            send([out(0, c)])
+        for t in SLOTS:
+            bs = [b for b in ORDER if _slot(b) == t]
+            for b in bs:
+                g.wait_ge(S["rl%d%d" % b], 1)
+            send([out(r, c) for r, c in bs])
+        finish()
+        return
+
+    r = T.rank_of(core)
+    if r is None:
+        return
+    pe, ve, sy, sc = g.tensor, g.vector, g.sync, g.scalar
+    wv, wh = T.m0[:, W:W + P], T.m0[:, W + P:W + 2 * P]
+    nldm = 0
+
+    def blk(c):
+        return slice(c * B, (c + 1) * B)
+
+    if r in HUBR:
+        for p in range(K // 2):
+            o = p * PAIRW
+            sy.dma_start(T.m0[:, o:o + W], T.x[:, 2 * p * W:(2 * p + 1) * W]).then_inc(S.ldm, 16)
+            sc.dma_start(T.m0[:, o + W + 2 * P:o + PAIRW], T.x[:, (2 * p + 1) * W:(2 * p + 2) * W]).then_inc(S.ldm, 16)
+            sy.dma_start(T.m0[:, o + W:o + W + P], T.wv[:, :]).then_inc(S.ldm, 16)
+            sc.dma_start(T.m0[:, o + W + P:o + W + 2 * P], T.wh[:, :]).then_inc(S.ldm, 16)
+            nldm += 64
+        for c in (1, 2, 0):
+            sy.dma_start(T.xin[:, blk(c)], T.x[:, blk(c)]).then_inc(S["ld%d" % c], 16)
+    else:
+        sy.dma_start(T.xin[:, blk(0)], T.x[:, blk(0)]).then_inc(S.ld0, 16)
+        sc.dma_start(wh, T.wh[:, :]).then_inc(S.ldm, 16)
+        nldm += 16
+        if r:
+            sc.dma_start(wv, T.wv[:, :]).then_inc(S.ldm, 16)
+            nldm += 16
+        for c in (1, 2):
+            sy.dma_start(T.xin[:, blk(c)], T.x[:, blk(c)]).then_inc(S["ld%d" % c], 16)
+    constants(sc)
+
+    if r in HUBR:
+        tos = relays[r] if r in relays else lanes
+        for c in range(NB):
+            g.wait_ge(S.ldm, nldm) if c == 0 else g.wait_ge(S["ld%d" % c], 16)
+            trs = []
+            for k in range(K):
+                m = _part(topo.mask(core, tos[k]), K, k)
+                if c == 0:
+                    a, b = msg_cols(k)
+                    src = T.m0[:, a:b]
+                    far = T.hubin[:, hub_region(r):hub_region(r) + MW]
+                else:
+                    src = T.xin[:, c * B + k * W:c * B + (k + 1) * W]
+                    o = hub_region(r) + 2 * P + c * W
+                    far = T.hubin[:, o:o + W]
+                if r in relays:
+                    trs.append(tr(tos[k], src, src, S["ah%d" % c], m))
+                else:
+                    trs.append(tr(tos[k], far, src, S["ax%d%d" % (r, c)], m))
+            send(trs)
+    if r == 0:
+        for c in range(NB):
+            for j in range(HS):
+                g.wait_ge(S["rl%d%d" % (j, c)], 1)
+            near = topo.mask(core, pass0) & ~topo.mask(core, lanes[0])
+            cols = [slice(c * B + k * W, c * B + (k + 1) * W) for k in range(K)]
+            send([tr(lanes[k], T.hubh[:, c * W:(c + 1) * W], T.hown[:, cols[k]], S["ax0%d" % c],
+                     _part(topo.mask(core, lanes[k]), K, k)) for k in range(K)]
+                 + [tr(pass0, T.hprev[:, cols[k]], T.hown[:, cols[k]], S["ah%d" % c], _part(near, K, k))
+                    for k in range(K) if c not in LANE_FWD])
+
+    def piece(c, j):
+        return slice(c * B + j * HW, c * B + (j + 1) * HW)
+
+    def acc(c, j):
+        i = c * HS + j
+        return T.ps[:, i * 512:i * 512 + HW]
+
+    def n_h(c):
+        if r == 1 and c not in LANE_FWD:
+            return len(_bits(topo.mask(pass0, core)))
+        return K * len(_bits(_out_masks(topo, lanes[0], R)[(r - 1, c)]))
+
+    pe.wait_ge(S.ldm, nldm)
+    pe.wait_ge(S.id2, 16)
+    for c in range(NB):
+        if r or c:
+            pe.wait_ge(S["ld%d" % c], 16)
+            for j in range(HS):
+                pe.matmul(acc(c, j), T.ident[:, :], T.xin[:, piece(c, j)], start=True, stop=False)
+    for c in range(NB):
+        if c:
+            for j in range(HS):
+                pe.wait_ge(S["rl%d%d" % (j, c - 1)], 1)
+                i = pe.matmul(acc(c, j), wh, T.hown[:, piece(c - 1, j)], start=False, stop=(r == 0))
+                if r == 0:
+                    i.then_inc(S["pe%d%d" % (j, c)], 1)
+        if r:
+            pe.wait_ge(S["ah%d" % c], n_h(c))
+            for j in range(HS):
+                pe.matmul(acc(c, j), wv, T.hprev[:, piece(c, j)], start=False, stop=True).then_inc(S["pe%d%d" % (j, c)], 1)
+    for c in range(NB):
+        for j in range(HS):
+            if r == 0 and c == 0:
+                if j == 0:
+                    ve.wait_ge(S.ld0, 16)
+                src = T.xin[:, piece(c, j)]
+            else:
+                ve.wait_ge(S["pe%d%d" % (j, c)], 1)
+                src = acc(c, j)
+            ve.tensor_tensor(out=T.hown[:, piece(c, j)], in0=src, in1=T.zeros[:, 0:HW], op=AluOpType.max).then_inc(S["rl%d%d" % (j, c)], 1)
+            q = (sy, sc)[j % 2]
+            q.wait_ge(S["rl%d%d" % (j, c)], 1)
+            q.dma_start(T.y[:, piece(c, j)], T.hown[:, piece(c, j)]).then_inc(S["st%d" % c], 16)
+    for c in range(NB):
+        g.wait_ge(S["st%d" % c], 16 * HS)
+    finish()

@@ -5,18 +5,16 @@ NSIM = 512
 P, B, NB = 128, 512, 3
 K = 2
 W = B // K
-MW = W + 2 * P
-PAIRW = 2 * W + 2 * P
 RW = 2 * P + NB * W
 HUBR = (1, 2, 3, 4)
 NBANK = 8
-RELAY_ALL = False
+RELAY_ALL = True
 LANE_FWD = (0,)
 HS = 2
 HW = B // HS
 
 SCRATCH = {
-    "m0": ("sbuf", [P, (K // 2) * PAIRW], "bfloat16"),
+    "m0": ("sbuf", [P, 2 * P], "bfloat16"),
     "xin": ("sbuf", [P, NB * B], "bfloat16"),
     "hprev": ("sbuf", [P, NB * B], "bfloat16"),
     "hown": ("sbuf", [P, NB * B], "bfloat16"),
@@ -28,7 +26,8 @@ SCRATCH = {
     "idd": ("dram", [P + 1, P], "bfloat16"),
     "ps": ("psum", [P, NBANK * 512], "float32"),
 }
-SEMAPHORES = (["ms0", "ms1", "ms2", "id1", "id2", "ldm", "ld0", "ld1", "ld2", "ah0", "ah1", "ah2", "st0", "st1", "st2", "sent"]
+SEMAPHORES = (["ms0", "ms1", "ms2", "id1", "id2", "ldm", "ld0", "ld1", "ld2", "ahw", "ah0", "ah1", "ah2", "st0", "st1", "st2", "sent"]
+              + ["aw%d" % r for r in range(5)]
               + ["ax%d%d" % (r, c) for r in range(5) for c in range(NB)]
               + ["pe%d%d" % (r, c) for r in range(5) for c in range(NB)]
               + ["rl%d%d" % (r, c) for r in range(5) for c in range(NB)])
@@ -90,11 +89,17 @@ def _plan(T, topo):
             cands = [c for c in _chip_cores(topo, R[r]) if c not in R and all(topo.may_write(c, l) for l in lanes)]
             relays[r] = _pick(topo, cands, [topo.die(l) for l in lanes])
     pass0 = _pick(topo, [c for c in _chip_cores(topo, R[0]) if c not in R and topo.may_write(c, R[1])], [topo.die(R[0])])[0]
-    return R, lanes, relays, pass0
+    help0 = {}
+    for k in range(K):
+        if topo.die(lanes[k]) != topo.die(R[0]):
+            cands = [c for c in _chip_cores(topo, R[0]) if c not in R and c != pass0 and c not in help0.values()
+                     and topo.may_write(c, lanes[k])]
+            help0[k] = _pick(topo, cands, [topo.die(lanes[k])])[0]
+    return R, lanes, relays, pass0, help0
 
 
 def rank_program(g, core, T, topo):
-    R, lanes, relays, pass0 = _plan(T, topo)
+    R, lanes, relays, pass0, help0 = _plan(T, topo)
     S = T.sem
     sent = [0]
 
@@ -121,38 +126,51 @@ def rank_program(g, core, T, topo):
         q.wait_ge(S.id1, 16)
         q.dma_start(T.ident[:, :], T.idd[0:P, :]).then_inc(S.id2, 16)
 
-    def hub_region(r):
-        return (r - 1) * RW
+    def hub_w(r):
+        o = (r - 1) * RW
+        return T.hubin[:, o:o + 2 * P]
 
-    def msg_cols(k):
-        o = (k // 2) * PAIRW + (k % 2) * W
-        return o, o + MW
+    def hub_x(r, c):
+        o = (r - 1) * RW + 2 * P + c * W
+        return T.hubin[:, o:o + W]
+
+    def lane_cols(c, k):
+        return slice(c * B + k * W, c * B + (k + 1) * W)
 
     def n_in(src, dst, parts):
         return len(_bits(topo.mask(src, dst))) // parts
+
+    far0 = topo.mask(R[0], lanes[0])
+    near0 = topo.mask(R[0], pass0) & ~far0
+    direct0 = [k for k in range(K) if k not in help0]
+    m_help0 = dict((k, _part(_part(near0, 2, 0), len(help0), i)) for i, k in enumerate(sorted(help0)))
+    m_pass0 = [_part(_part(near0, 2, 1), K, k) for k in range(K)]
 
     for r in relays:
         if core in relays[r]:
             k = relays[r].index(core)
             lane = lanes[k]
             m = topo.mask(core, lane)
+            g.wait_ge(S.ahw, n_in(R[r], core, K))
+            send([tr(lane, hub_w(r), T.m0[:, :], S["aw%d" % r], m)])
             for c in range(NB):
                 g.wait_ge(S["ah%d" % c], n_in(R[r], core, K))
-                if c == 0:
-                    a, b = msg_cols(k)
-                    src, dst = T.m0[:, a:b], T.hubin[:, hub_region(r):hub_region(r) + MW]
-                else:
-                    o = hub_region(r) + 2 * P + c * W
-                    src, dst = T.xin[:, c * B + k * W:c * B + (k + 1) * W], T.hubin[:, o:o + W]
-                send([tr(lane, dst, src, S["ax%d%d" % (r, c)], m)])
+                send([tr(lane, hub_x(r, c), T.xin[:, lane_cols(c, k)], S["ax%d%d" % (r, c)], m)])
+            finish()
+            return
+
+    for k in help0:
+        if core == help0[k]:
+            for c in range(NB):
+                g.wait_ge(S["ah%d" % c], len(_bits(m_help0[k])))
+                send([tr(lanes[k], T.hubh[:, c * W:(c + 1) * W], T.hown[:, lane_cols(c, k)], S["ax0%d" % c], topo.mask(core, lanes[k]))])
             finish()
             return
 
     if core == pass0:
-        m_in = topo.mask(R[0], core) & ~topo.mask(R[0], lanes[0])
         for c in range(NB):
             if c not in LANE_FWD:
-                g.wait_ge(S["ah%d" % c], len(_bits(m_in)))
+                g.wait_ge(S["ah%d" % c], sum(len(_bits(m)) for m in m_pass0))
                 blk = slice(c * B, (c + 1) * B)
                 send([tr(R[1], T.hprev[:, blk], T.hprev[:, blk], S["ah%d" % c], topo.mask(core, R[1]))])
         finish()
@@ -160,35 +178,37 @@ def rank_program(g, core, T, topo):
 
     if core in lanes:
         k = lanes.index(core)
-        side = k % 2
         pe, ve = g.tensor, g.vector
         constants(g.sync)
 
-        def X(r, c):
-            o = hub_region(r) + (0 if (c == 0 and side == 0) else 2 * P + c * W)
-            return T.hubin[:, o:o + W]
-
         def WV(r):
-            o = hub_region(r) + (W if side == 0 else 0)
+            o = (r - 1) * RW
             return T.hubin[:, o:o + P]
 
         def WH(r):
-            o = hub_region(r) + (W if side == 0 else 0) + P
+            o = (r - 1) * RW + P
             return T.hubin[:, o:o + P]
 
         def H(r, c):
             o = (NB * r + c) * W
             return T.hubh[:, o:o + W]
 
-        bank, owner, has_a = {}, [None] * NBANK, set()
+        bank, owner, has_a, has_w = {}, [None] * NBANK, set(), set()
 
         def PS(b):
             return T.ps[:, bank[b] * 512:bank[b] * 512 + W]
 
         def n_arr(r):
+            if r == 0:
+                return len(_bits(topo.mask(help0[k], core))) if k in help0 else len(_bits(far0)) // len(direct0)
             if r in relays:
                 return len(_bits(topo.mask(relays[r][k], core)))
             return n_in(R[r], core, K)
+
+        def need_w(r):
+            if r not in has_w:
+                has_w.add(r)
+                pe.wait_ge(S["aw%d" % r], n_arr(r))
 
         def emit_a(b):
             if b in has_a:
@@ -202,16 +222,18 @@ def rank_program(g, core, T, topo):
                 pe.wait_ge(S["rl%d%d" % owner[i]], 1)
             owner[i], bank[b] = b, i
             pe.wait_ge(S["ax%d%d" % b], n_arr(b[0]))
-            pe.matmul(PS(b), T.ident[:, :], X(*b), start=True, stop=False)
+            pe.matmul(PS(b), T.ident[:, :], hub_x(*b), start=True, stop=False)
 
         def emit_c(b):
             r, c = b
             if c:
+                need_w(r)
                 pe.wait_ge(S["rl%d%d" % (r, c - 1)], 1)
                 pe.matmul(PS(b), WH(r), H(r, c - 1), start=False, stop=False)
 
         def emit_b(b):
             r, c = b
+            need_w(r)
             if r == 1:
                 pe.wait_ge(S["ax0%d" % c], n_arr(0))
             else:
@@ -240,7 +262,7 @@ def rank_program(g, core, T, topo):
         om = _out_masks(topo, core, R)
 
         def out(r, c):
-            return tr(R[r + 1], T.hprev[:, c * B + k * W:c * B + (k + 1) * W], H(r, c), S["ah%d" % c], om[(r, c)])
+            return tr(R[r + 1], T.hprev[:, lane_cols(c, k)], H(r, c), S["ah%d" % c], om[(r, c)])
 
         for c in LANE_FWD:
             g.wait_ge(S["ax0%d" % c], n_arr(0))
@@ -257,62 +279,49 @@ def rank_program(g, core, T, topo):
     if r is None:
         return
     pe, ve, sy, sc = g.tensor, g.vector, g.sync, g.scalar
-    wv, wh = T.m0[:, W:W + P], T.m0[:, W + P:W + 2 * P]
-    nldm = 0
+    wv, wh = T.m0[:, 0:P], T.m0[:, P:2 * P]
+    nldm = 16
 
     def blk(c):
         return slice(c * B, (c + 1) * B)
 
-    if r in HUBR:
-        for p in range(K // 2):
-            o = p * PAIRW
-            sy.dma_start(T.m0[:, o:o + W], T.x[:, 2 * p * W:(2 * p + 1) * W]).then_inc(S.ldm, 16)
-            sc.dma_start(T.m0[:, o + W + 2 * P:o + PAIRW], T.x[:, (2 * p + 1) * W:(2 * p + 2) * W]).then_inc(S.ldm, 16)
-            sy.dma_start(T.m0[:, o + W:o + W + P], T.wv[:, :]).then_inc(S.ldm, 16)
-            sc.dma_start(T.m0[:, o + W + P:o + W + 2 * P], T.wh[:, :]).then_inc(S.ldm, 16)
-            nldm += 64
-        for c in (1, 2, 0):
-            sy.dma_start(T.xin[:, blk(c)], T.x[:, blk(c)]).then_inc(S["ld%d" % c], 16)
+    def load(q, c):
+        q.dma_start(T.xin[:, blk(c)], T.x[:, blk(c)]).then_inc(S["ld%d" % c], 16)
+
+    if r == 0:
+        load(sy, 0)
+        sc.dma_start(wh, T.wh[:, :]).then_inc(S.ldm, 16)
     else:
-        sy.dma_start(T.xin[:, blk(0)], T.x[:, blk(0)]).then_inc(S.ld0, 16)
+        sy.dma_start(wv, T.wv[:, :]).then_inc(S.ldm, 16)
         sc.dma_start(wh, T.wh[:, :]).then_inc(S.ldm, 16)
         nldm += 16
-        if r:
-            sc.dma_start(wv, T.wv[:, :]).then_inc(S.ldm, 16)
-            nldm += 16
-        for c in (1, 2):
-            sy.dma_start(T.xin[:, blk(c)], T.x[:, blk(c)]).then_inc(S["ld%d" % c], 16)
+        load(sy, 0)
+    load(sc, 1)
+    load(sy, 2)
     constants(sc)
 
     if r in HUBR:
         tos = relays[r] if r in relays else lanes
+        ms = [_part(topo.mask(core, tos[k]), K, k) for k in range(K)]
+        g.wait_ge(S.ldm, nldm)
+        if r in relays:
+            send([tr(tos[k], T.m0[:, :], T.m0[:, :], S.ahw, ms[k]) for k in range(K)])
+        else:
+            send([tr(tos[k], hub_w(r), T.m0[:, :], S["aw%d" % r], ms[k]) for k in range(K)])
         for c in range(NB):
-            g.wait_ge(S.ldm, nldm) if c == 0 else g.wait_ge(S["ld%d" % c], 16)
-            trs = []
-            for k in range(K):
-                m = _part(topo.mask(core, tos[k]), K, k)
-                if c == 0:
-                    a, b = msg_cols(k)
-                    src = T.m0[:, a:b]
-                    far = T.hubin[:, hub_region(r):hub_region(r) + MW]
-                else:
-                    src = T.xin[:, c * B + k * W:c * B + (k + 1) * W]
-                    o = hub_region(r) + 2 * P + c * W
-                    far = T.hubin[:, o:o + W]
-                if r in relays:
-                    trs.append(tr(tos[k], src, src, S["ah%d" % c], m))
-                else:
-                    trs.append(tr(tos[k], far, src, S["ax%d%d" % (r, c)], m))
-            send(trs)
+            g.wait_ge(S["ld%d" % c], 16)
+            if r in relays:
+                send([tr(tos[k], T.xin[:, lane_cols(c, k)], T.xin[:, lane_cols(c, k)], S["ah%d" % c], ms[k]) for k in range(K)])
+            else:
+                send([tr(tos[k], hub_x(r, c), T.xin[:, lane_cols(c, k)], S["ax%d%d" % (r, c)], ms[k]) for k in range(K)])
     if r == 0:
         for c in range(NB):
             for j in range(HS):
                 g.wait_ge(S["rl%d%d" % (j, c)], 1)
-            near = topo.mask(core, pass0) & ~topo.mask(core, lanes[0])
-            cols = [slice(c * B + k * W, c * B + (k + 1) * W) for k in range(K)]
-            send([tr(lanes[k], T.hubh[:, c * W:(c + 1) * W], T.hown[:, cols[k]], S["ax0%d" % c],
-                     _part(topo.mask(core, lanes[k]), K, k)) for k in range(K)]
-                 + [tr(pass0, T.hprev[:, cols[k]], T.hown[:, cols[k]], S["ah%d" % c], _part(near, K, k))
+            send([tr(lanes[k], T.hubh[:, c * W:(c + 1) * W], T.hown[:, lane_cols(c, k)], S["ax0%d" % c],
+                     _part(far0, len(direct0), i)) for i, k in enumerate(direct0)]
+                 + [tr(help0[k], T.hown[:, lane_cols(c, k)], T.hown[:, lane_cols(c, k)], S["ah%d" % c], m_help0[k]) for k in sorted(help0)]
+                 + [tr(pass0, T.hprev[:, lane_cols(c, k)], T.hown[:, lane_cols(c, k)], S["ah%d" % c], m_pass0[k])
                     for k in range(K) if c not in LANE_FWD])
 
     def piece(c, j):

@@ -87,19 +87,23 @@ def _plan(T, topo):
         here = topo.host(R[r]) == topo.host(lanes[0]) and topo.chip(R[r]) == topo.chip(lanes[0])
         if not all(topo.may_write(R[r], l) for l in lanes) or (RELAY_ALL and not here):
             cands = [c for c in _chip_cores(topo, R[r]) if c not in R and all(topo.may_write(c, l) for l in lanes)]
-            relays[r] = _pick(topo, cands, [topo.die(l) for l in lanes])
-    pass0 = _pick(topo, [c for c in _chip_cores(topo, R[0]) if c not in R and topo.may_write(c, R[1])], [topo.die(R[0])])[0]
-    help0 = {}
-    for k in range(K):
-        if topo.die(lanes[k]) != topo.die(R[0]):
-            cands = [c for c in _chip_cores(topo, R[0]) if c not in R and c != pass0 and c not in help0.values()
-                     and topo.may_write(c, lanes[k])]
-            help0[k] = _pick(topo, cands, [topo.die(lanes[k])])[0]
-    return R, lanes, relays, pass0, help0
+            door = [c for c in range(NSIM) if topo.mates(c, lanes[0]) and topo.same_plane(R[r], c) and topo.may_write(R[r], c)
+                    and all(topo.may_write(c, l) for l in lanes)]
+            relays[r] = _pick(topo, door or cands, [topo.die(l) for l in lanes])
+    ports0 = [c for c in _chip_cores(topo, R[0]) if c not in R and topo.may_write(c, R[1])]
+    help0 = dict(enumerate(_pick(topo, ports0, [topo.die(l) for l in lanes])))
+    pass0 = _pick(topo, [c for c in ports0 if c not in help0.values()], [topo.die(R[0])])[0]
+    wdoor = {}
+    for r in relays:
+        if topo.rack(topo.host(R[r])) != topo.rack(topo.host(lanes[0])):
+            cands = [c for c in range(NSIM) if topo.host(c) == topo.host(lanes[0]) and topo.chip(c) == topo.chip(R[r]) and c not in R
+                     and topo.may_write(R[r], c) and all(topo.may_write(c, l) for l in lanes)]
+            wdoor[r] = _pick(topo, cands, [topo.die(R[r])])[0]
+    return R, lanes, relays, pass0, help0, wdoor
 
 
 def rank_program(g, core, T, topo):
-    R, lanes, relays, pass0, help0 = _plan(T, topo)
+    R, lanes, relays, pass0, help0, wdoor = _plan(T, topo)
     S = T.sem
     sent = [0]
 
@@ -140,22 +144,28 @@ def rank_program(g, core, T, topo):
     def n_in(src, dst, parts):
         return len(_bits(topo.mask(src, dst))) // parts
 
-    far0 = topo.mask(R[0], lanes[0])
-    near0 = topo.mask(R[0], pass0) & ~far0
-    direct0 = [k for k in range(K) if k not in help0]
-    m_help0 = dict((k, _part(_part(near0, 2, 0), len(help0), i)) for i, k in enumerate(sorted(help0)))
-    m_pass0 = [_part(_part(near0, 2, 1), K, k) for k in range(K)]
+    all0 = topo.mask(R[0], pass0)
+    m_help0 = dict((k, _part(all0, 2 * K, k)) for k in range(K))
+    m_pass0 = [_part(all0, 2 * K, K + k) for k in range(K)]
 
     for r in relays:
         if core in relays[r]:
             k = relays[r].index(core)
             lane = lanes[k]
             m = topo.mask(core, lane)
-            g.wait_ge(S.ahw, n_in(R[r], core, K))
-            send([tr(lane, hub_w(r), T.m0[:, :], S["aw%d" % r], m)])
+            if r not in wdoor:
+                g.wait_ge(S.ahw, n_in(R[r], core, K))
+                send([tr(lane, hub_w(r), T.m0[:, :], S["aw%d" % r], m)])
             for c in range(NB):
                 g.wait_ge(S["ah%d" % c], n_in(R[r], core, K))
                 send([tr(lane, hub_x(r, c), T.xin[:, lane_cols(c, k)], S["ax%d%d" % (r, c)], m)])
+            finish()
+            return
+
+    for r in wdoor:
+        if core == wdoor[r]:
+            g.wait_ge(S.ahw, n_in(R[r], core, 1))
+            send([tr(lanes[k], hub_w(r), T.m0[:, :], S["aw%d" % r], _part(topo.mask(core, lanes[k]), K, k)) for k in range(K)])
             finish()
             return
 
@@ -200,7 +210,7 @@ def rank_program(g, core, T, topo):
 
         def n_arr(r):
             if r == 0:
-                return len(_bits(topo.mask(help0[k], core))) if k in help0 else len(_bits(far0)) // len(direct0)
+                return len(_bits(topo.mask(help0[k], core)))
             if r in relays:
                 return len(_bits(topo.mask(relays[r][k], core)))
             return n_in(R[r], core, K)
@@ -208,7 +218,7 @@ def rank_program(g, core, T, topo):
         def need_w(r):
             if r not in has_w:
                 has_w.add(r)
-                pe.wait_ge(S["aw%d" % r], n_arr(r))
+                pe.wait_ge(S["aw%d" % r], n_in(wdoor[r], core, K) if r in wdoor else n_arr(r))
 
         def emit_a(b):
             if b in has_a:
@@ -241,8 +251,7 @@ def rank_program(g, core, T, topo):
             pe.matmul(PS(b), WV(r), H(r - 1, c), start=False, stop=True).then_inc(S["pe%d%d" % b], 1)
 
         pe.wait_ge(S.id2, 16)
-        early = [(r, c) for r in HUBR if r not in relays and topo.chip(R[r]) == topo.chip(core) and topo.host(R[r]) == topo.host(core)
-                 for c in range(NB)] + [(r, 0) for r in HUBR if r not in relays]
+        early = [(r, c) for r in HUBR if r not in relays for c in range(NB)]
         for b in early:
             emit_a(b)
         for b in ORDER:
@@ -304,7 +313,9 @@ def rank_program(g, core, T, topo):
         tos = relays[r] if r in relays else lanes
         ms = [_part(topo.mask(core, tos[k]), K, k) for k in range(K)]
         g.wait_ge(S.ldm, nldm)
-        if r in relays:
+        if r in wdoor:
+            send([tr(wdoor[r], T.m0[:, :], T.m0[:, :], S.ahw, topo.mask(core, wdoor[r]))])
+        elif r in relays:
             send([tr(tos[k], T.m0[:, :], T.m0[:, :], S.ahw, ms[k]) for k in range(K)])
         else:
             send([tr(tos[k], hub_w(r), T.m0[:, :], S["aw%d" % r], ms[k]) for k in range(K)])
@@ -318,9 +329,7 @@ def rank_program(g, core, T, topo):
         for c in range(NB):
             for j in range(HS):
                 g.wait_ge(S["rl%d%d" % (j, c)], 1)
-            send([tr(lanes[k], T.hubh[:, c * W:(c + 1) * W], T.hown[:, lane_cols(c, k)], S["ax0%d" % c],
-                     _part(far0, len(direct0), i)) for i, k in enumerate(direct0)]
-                 + [tr(help0[k], T.hown[:, lane_cols(c, k)], T.hown[:, lane_cols(c, k)], S["ah%d" % c], m_help0[k]) for k in sorted(help0)]
+            send([tr(help0[k], T.hown[:, lane_cols(c, k)], T.hown[:, lane_cols(c, k)], S["ah%d" % c], m_help0[k]) for k in sorted(help0)]
                  + [tr(pass0, T.hprev[:, lane_cols(c, k)], T.hown[:, lane_cols(c, k)], S["ah%d" % c], m_pass0[k])
                     for k in range(K) if c not in LANE_FWD])
 

from concourse.bass import DstId, RemoteDMATransfer
from concourse.mybir import AluOpType

NSIM = 512
P, B, NB = 128, 512, 3
K = 2
W = B // K
RW = 2 * P + NB * W
HUBR = (1, 2, 3, 4)
NBANK = 8
RELAY_ALL = True
LANE_FWD = (0,)
HS = 2
HW = B // HS

SCRATCH = {
    "m0": ("sbuf", [P, 2 * P], "bfloat16"),
    "xin": ("sbuf", [P, NB * B], "bfloat16"),
    "hprev": ("sbuf", [P, NB * B], "bfloat16"),
    "hown": ("sbuf", [P, NB * B], "bfloat16"),
    "ident": ("sbuf", [P, P], "bfloat16"),
    "idsrc": ("sbuf", [P, P + 1], "bfloat16"),
    "zeros": ("sbuf", [P, B], "bfloat16"),
    "hubin": ("sbuf", [P, len(HUBR) * RW], "bfloat16"),
    "hubh": ("sbuf", [P, (len(HUBR) + 1) * NB * W], "bfloat16"),
    "idd": ("dram", [P + 1, P], "bfloat16"),
    "ps": ("psum", [P, NBANK * 512], "float32"),
}
SEMAPHORES = (["ms0", "ms1", "ms2", "id1", "id2", "ldm", "ld0", "ld1", "ld2", "ahw", "ah0", "ah1", "ah2", "st0", "st1", "st2", "sent"]
              + ["aw%d" % r for r in range(5)]
              + ["ax%d%d" % (r, c) for r in range(5) for c in range(NB)]
              + ["pe%d%d" % (r, c) for r in range(5) for c in range(NB)]
              + ["rl%d%d" % (r, c) for r in range(5) for c in range(NB)])


def _bits(m):
    return [i for i in range(16) if (m >> i) & 1]


def _mask(lst):
    return sum(1 << i for i in lst)


def _part(m, n, j):
    b = _bits(m)
    q = len(b) // n
    return _mask(b[j * q:(j + 1) * q])


def _chip_cores(topo, c):
    return [d for d in range(NSIM) if topo.host(d) == topo.host(c) and topo.chip(d) == topo.chip(c)]


def _pick(topo, cands, dies):
    out = []
    for d in dies:
        out.append([c for c in cands if topo.die(c) == d and c not in out][0])
    return out


def _slot(b):
    return 2 * b[1] + b[0]


ORDER = sorted([(r, c) for r in HUBR for c in range(NB)], key=lambda b: (_slot(b), b[1]))
SLOTS = sorted(set(_slot(b) for b in ORDER))


def _out_masks(topo, lane, R):
    off = topo.mask(lane, R[HUBR[-1] + 1])
    out = dict(((0, c), off) for c in LANE_FWD)
    for t in SLOTS:
        bs = [b for b in ORDER if _slot(b) == t]
        far = [b for b in bs if not (topo.mask(lane, R[b[0] + 1]) & ~off)]
        for b in bs:
            out[b] = _part(off, len(far), far.index(b)) if b in far else topo.mask(lane, R[b[0] + 1]) & ~off
    return out


def _plan(T, topo):
    R = list(T.cores)
    own = [c for c in _chip_cores(topo, R[2]) if c not in R and all(topo.may_write(c, R[r + 1]) for r in (0,) + HUBR)]
    dies = sorted(set(topo.die(c) for c in own), key=lambda d: d != topo.die(R[2]))
    lanes = _pick(topo, own, [dies[k % len(dies)] for k in range(K)])
    relays = {}
    for r in HUBR:
        here = topo.host(R[r]) == topo.host(lanes[0]) and topo.chip(R[r]) == topo.chip(lanes[0])
        if not all(topo.may_write(R[r], l) for l in lanes) or (RELAY_ALL and not here):
            cands = [c for c in _chip_cores(topo, R[r]) if c not in R and all(topo.may_write(c, l) for l in lanes)]
            door = [c for c in range(NSIM) if topo.mates(c, lanes[0]) and topo.same_plane(R[r], c) and topo.may_write(R[r], c)
                    and all(topo.may_write(c, l) for l in lanes)]
            relays[r] = _pick(topo, door or cands, [topo.die(l) for l in lanes])
    ports0 = [c for c in _chip_cores(topo, R[0]) if c not in R and topo.may_write(c, R[1])]
    help0 = dict(enumerate(_pick(topo, ports0, [topo.die(l) for l in lanes])))
    pass0 = _pick(topo, [c for c in ports0 if c not in help0.values()], [topo.die(R[0])])[0]
    wdoor = {}
    for r in relays:
        if topo.rack(topo.host(R[r])) != topo.rack(topo.host(lanes[0])):
            cands = [c for c in range(NSIM) if topo.host(c) == topo.host(lanes[0]) and topo.chip(c) == topo.chip(R[r]) and c not in R
                     and topo.may_write(R[r], c) and all(topo.may_write(c, l) for l in lanes)]
            wdoor[r] = _pick(topo, cands, [topo.die(R[r])])[0]
    return R, lanes, relays, pass0, help0, wdoor


def rank_program(g, core, T, topo):
    R, lanes, relays, pass0, help0, wdoor = _plan(T, topo)
    S = T.sem
    sent = [0]

    def tr(dst, out_ap, in_ap, sem, mask):
        rid, pid = topo.addr(dst, core)
        sent[0] += len(_bits(mask))
        return RemoteDMATransfer(dst_ids=[DstId(rid=rid, pnc=pid)], dma_engine_mask=mask, remote_sem=sem, src=in_ap, dst=out_ap)

    def send(trs):
        g.remote_dma_fused(trs, local_sem=S.sent)

    def finish():
        if sent[0]:
            g.wait_ge(S.sent, sent[0])

    def constants(q):
        g.vector.memset(T.idsrc[:, :], 0.0).then_inc(S.ms0, 1)
        g.vector.wait_ge(S.ms0, 1)
        g.vector.memset(T.idsrc[:, 0:1], 1.0).then_inc(S.ms1, 1)
        g.vector.memset(T.zeros[:, :], 0.0).then_inc(S.ms2, 1)
        g.vector.wait_ge(S.ms2, 1)
        q.wait_ge(S.ms1, 1)
        q.dma_start(T.idd[:, :], T.idsrc[:, :]).then_inc(S.id1, 16)
        q.wait_ge(S.id1, 16)
        q.dma_start(T.ident[:, :], T.idd[0:P, :]).then_inc(S.id2, 16)

    def hub_w(r):
        o = (r - 1) * RW
        return T.hubin[:, o:o + 2 * P]

    def hub_x(r, c):
        o = (r - 1) * RW + 2 * P + c * W
        return T.hubin[:, o:o + W]

    def lane_cols(c, k):
        return slice(c * B + k * W, c * B + (k + 1) * W)

    def n_in(src, dst, parts):
        return len(_bits(topo.mask(src, dst))) // parts

    all0 = topo.mask(R[0], pass0)
    m_help0 = dict((k, _part(all0, 2 * K, k)) for k in range(K))
    m_pass0 = [_part(all0, 2 * K, K + k) for k in range(K)]

    for r in relays:
        if core in relays[r]:
            k = relays[r].index(core)
            lane = lanes[k]
            m = topo.mask(core, lane)
            if r not in wdoor:
                g.wait_ge(S.ahw, n_in(R[r], core, K))
                send([tr(lane, hub_w(r), T.m0[:, :], S["aw%d" % r], m)])
            for c in range(NB):
                g.wait_ge(S["ah%d" % c], n_in(R[r], core, K))
                send([tr(lane, hub_x(r, c), T.xin[:, lane_cols(c, k)], S["ax%d%d" % (r, c)], m)])
            finish()
            return

    for r in wdoor:
        if core == wdoor[r]:
            g.wait_ge(S.ahw, n_in(R[r], core, 1))
            send([tr(lanes[k], hub_w(r), T.m0[:, :], S["aw%d" % r], _part(topo.mask(core, lanes[k]), K, k)) for k in range(K)])
            finish()
            return

    for k in help0:
        if core == help0[k]:
            for c in range(NB):
                g.wait_ge(S["ah%d" % c], len(_bits(m_help0[k])))
                send([tr(lanes[k], T.hubh[:, c * W:(c + 1) * W], T.hown[:, lane_cols(c, k)], S["ax0%d" % c], topo.mask(core, lanes[k]))])
            finish()
            return

    if core == pass0:
        for c in range(NB):
            if c not in LANE_FWD:
                g.wait_ge(S["ah%d" % c], sum(len(_bits(m)) for m in m_pass0))
                blk = slice(c * B, (c + 1) * B)
                send([tr(R[1], T.hprev[:, blk], T.hprev[:, blk], S["ah%d" % c], topo.mask(core, R[1]))])
        finish()
        return

    if core in lanes:
        k = lanes.index(core)
        pe, ve = g.tensor, g.vector
        constants(g.sync)

        def WV(r):
            o = (r - 1) * RW
            return T.hubin[:, o:o + P]

        def WH(r):
            o = (r - 1) * RW + P
            return T.hubin[:, o:o + P]

        def H(r, c):
            o = (NB * r + c) * W
            return T.hubh[:, o:o + W]

        bank, owner, has_a, has_w = {}, [None] * NBANK, set(), set()

        def PS(b):
            return T.ps[:, bank[b] * 512:bank[b] * 512 + W]

        def n_arr(r):
            if r == 0:
                return len(_bits(topo.mask(help0[k], core)))
            if r in relays:
                return len(_bits(topo.mask(relays[r][k], core)))
            return n_in(R[r], core, K)

        def need_w(r):
            if r not in has_w:
                has_w.add(r)
                pe.wait_ge(S["aw%d" % r], n_in(wdoor[r], core, K) if r in wdoor else n_arr(r))

        def emit_a(b):
            if b in has_a:
                return
            has_a.add(b)
            free = [i for i in range(NBANK) if owner[i] is None]
            if free:
                i = free[0]
            else:
                i = min(range(NBANK), key=lambda j: ORDER.index(owner[j]))
                pe.wait_ge(S["rl%d%d" % owner[i]], 1)
            owner[i], bank[b] = b, i
            pe.wait_ge(S["ax%d%d" % b], n_arr(b[0]))
            pe.matmul(PS(b), T.ident[:, :], hub_x(*b), start=True, stop=False)

        def emit_c(b):
            r, c = b
            if c:
                need_w(r)
                pe.wait_ge(S["rl%d%d" % (r, c - 1)], 1)
                pe.matmul(PS(b), WH(r), H(r, c - 1), start=False, stop=False)

        def emit_b(b):
            r, c = b
            need_w(r)
            if r == 1:
                pe.wait_ge(S["ax0%d" % c], n_arr(0))
            else:
                pe.wait_ge(S["rl%d%d" % (r - 1, c)], 1)
            pe.matmul(PS(b), WV(r), H(r - 1, c), start=False, stop=True).then_inc(S["pe%d%d" % b], 1)

        pe.wait_ge(S.id2, 16)
        early = [(r, c) for r in HUBR if r not in relays for c in range(NB)]
        for b in early:
            emit_a(b)
        for b in ORDER:
            if _slot(b) == SLOTS[0]:
                emit_a(b)
        for t in SLOTS:
            for b in ORDER:
                if _slot(b) == t:
                    emit_b(b)
            for b in ORDER:
                if _slot(b) == t + 1:
                    emit_a(b)
                    emit_c(b)
        for b in ORDER:
            ve.wait_ge(S["pe%d%d" % b], 1)
            ve.tensor_tensor(out=H(*b), in0=PS(b), in1=T.zeros[:, 0:W], op=AluOpType.max).then_inc(S["rl%d%d" % b], 1)
        om = _out_masks(topo, core, R)

        def out(r, c):
            return tr(R[r + 1], T.hprev[:, lane_cols(c, k)], H(r, c), S["ah%d" % c], om[(r, c)])

        for c in LANE_FWD:
            g.wait_ge(S["ax0%d" % c], n_arr(0))
            send([out(0, c)])
        for t in SLOTS:
            bs = [b for b in ORDER if _slot(b) == t]
            for b in bs:
                g.wait_ge(S["rl%d%d" % b], 1)
            send([out(r, c) for r, c in bs])
        finish()
        return

    r = T.rank_of(core)
    if r is None:
        return
    pe, ve, sy, sc = g.tensor, g.vector, g.sync, g.scalar
    wv, wh = T.m0[:, 0:P], T.m0[:, P:2 * P]
    nldm = 16

    def blk(c):
        return slice(c * B, (c + 1) * B)

    def load(q, c):
        q.dma_start(T.xin[:, blk(c)], T.x[:, blk(c)]).then_inc(S["ld%d" % c], 16)

    if r == 0:
        load(sy, 0)
        sc.dma_start(wh, T.wh[:, :]).then_inc(S.ldm, 16)
    else:
        sy.dma_start(wv, T.wv[:, :]).then_inc(S.ldm, 16)
        sc.dma_start(wh, T.wh[:, :]).then_inc(S.ldm, 16)
        nldm += 16
        load(sy, 0)
    load(sc, 1)
    load(sy, 2)
    constants(sc)

    if r in HUBR:
        tos = relays[r] if r in relays else lanes
        ms = [_part(topo.mask(core, tos[k]), K, k) for k in range(K)]
        g.wait_ge(S.ldm, nldm)
        if r in wdoor:
            send([tr(wdoor[r], T.m0[:, :], T.m0[:, :], S.ahw, topo.mask(core, wdoor[r]))])
        elif r in relays:
            send([tr(tos[k], T.m0[:, :], T.m0[:, :], S.ahw, ms[k]) for k in range(K)])
        else:
            send([tr(tos[k], hub_w(r), T.m0[:, :], S["aw%d" % r], ms[k]) for k in range(K)])
        for c in range(NB):
            g.wait_ge(S["ld%d" % c], 16)
            if r in relays:
                send([tr(tos[k], T.xin[:, lane_cols(c, k)], T.xin[:, lane_cols(c, k)], S["ah%d" % c], ms[k]) for k in range(K)])
            else:
                send([tr(tos[k], hub_x(r, c), T.xin[:, lane_cols(c, k)], S["ax%d%d" % (r, c)], ms[k]) for k in range(K)])
    if r == 0:
        for c in range(NB):
            for j in range(HS):
                g.wait_ge(S["rl%d%d" % (j, c)], 1)
            send([tr(help0[k], T.hown[:, lane_cols(c, k)], T.hown[:, lane_cols(c, k)], S["ah%d" % c], m_help0[k]) for k in sorted(help0)]
                 + [tr(pass0, T.hprev[:, lane_cols(c, k)], T.hown[:, lane_cols(c, k)], S["ah%d" % c], m_pass0[k])
                    for k in range(K) if c not in LANE_FWD])

    def piece(c, j):
        return slice(c * B + j * HW, c * B + (j + 1) * HW)

    def acc(c, j):
        i = c * HS + j
        return T.ps[:, i * 512:i * 512 + HW]

    def n_h(c):
        if r == 1 and c not in LANE_FWD:
            return len(_bits(topo.mask(pass0, core)))
        return K * len(_bits(_out_masks(topo, lanes[0], R)[(r - 1, c)]))

    pe.wait_ge(S.ldm, nldm)
    pe.wait_ge(S.id2, 16)
    for c in range(NB):
        if r or c:
            pe.wait_ge(S["ld%d" % c], 16)
            for j in range(HS):
                pe.matmul(acc(c, j), T.ident[:, :], T.xin[:, piece(c, j)], start=True, stop=False)
    for c in range(NB):
        if c:
            for j in range(HS):
                pe.wait_ge(S["rl%d%d" % (j, c - 1)], 1)
                i = pe.matmul(acc(c, j), wh, T.hown[:, piece(c - 1, j)], start=False, stop=(r == 0))
                if r == 0:
                    i.then_inc(S["pe%d%d" % (j, c)], 1)
        if r:
            pe.wait_ge(S["ah%d" % c], n_h(c))
            for j in range(HS):
                pe.matmul(acc(c, j), wv, T.hprev[:, piece(c, j)], start=False, stop=True).then_inc(S["pe%d%d" % (j, c)], 1)
    for c in range(NB):
        for j in range(HS):
            if r == 0 and c == 0:
                if j == 0:
                    ve.wait_ge(S.ld0, 16)
                src = T.xin[:, piece(c, j)]
            else:
                ve.wait_ge(S["pe%d%d" % (j, c)], 1)
                src = acc(c, j)
            ve.tensor_tensor(out=T.hown[:, piece(c, j)], in0=src, in1=T.zeros[:, 0:HW], op=AluOpType.max).then_inc(S["rl%d%d" % (j, c)], 1)
            q = (sy, sc)[j % 2]
            q.wait_ge(S["rl%d%d" % (j, c)], 1)
            q.dma_start(T.y[:, piece(c, j)], T.hown[:, piece(c, j)]).then_inc(S["st%d" % c], 16)
    for c in range(NB):
        g.wait_ge(S["st%d" % c], 16 * HS)
    finish()
